import numpy as np
import ml_dtypes


def mxq(x, axis, fmt="e4m3"):
    dtype, down = {"e4m3": (ml_dtypes.float8_e4m3fn, 7), "e5m2": (ml_dtypes.float8_e5m2, 14)}[fmt]
    v = np.moveaxis(np.asarray(x, np.float32).astype(ml_dtypes.bfloat16).astype(np.float64), axis, -1)
    blocks = v.reshape(v.shape[:-1] + (-1, 32))
    amax = np.abs(blocks).max(-1, keepdims=True)
    byte = np.maximum(np.where(amax > 0, np.frexp(amax)[1] - 1 + 127, 0) - down, 1)
    scale = np.exp2(byte - 127.0)
    codes = (blocks / scale).astype(np.float32).astype(dtype).astype(np.float64)
    return np.moveaxis((codes * scale).reshape(v.shape), -1, axis)


WIDE = False


def mx_kscale(k):
    if not WIDE:
        return np.ones(k)
    levels = np.array([10, -10, 5, -5, 0])
    if k % 512:
        return np.exp2(np.random.permutation(np.resize(levels, k // 32))).repeat(32)
    a = np.empty((k // 512, 16))
    for p in range(k // 512):
        a[p, :8] = np.random.permutation(np.resize(levels, 8))
        for g in range(8):
            far = levels[np.abs(levels - a[p, g]) >= 10]
            a[p, g + 8] = far[np.random.randint(len(far))]
    return np.exp2(a.ravel()).repeat(32)


def f64(x):
    return np.asarray(x).astype(np.float64)


def striped(idx):
    return np.tile(np.asarray(idx).reshape(-1, 16).T, (8, 1)).astype(np.uint16)


def unstriped(offs):
    return offs[:16].T.reshape(-1).astype(np.int64)


E2M1 = np.array([0.0, 0.5, 1.0, 1.5, 2.0, 3.0, 4.0, 6.0, -0.0, -0.5, -1.0, -1.5, -2.0, -3.0, -4.0, -6.0])


def pack_weight(w, fmt):
    k, n = w.shape
    w = f64(np.asarray(w, np.float32).astype(ml_dtypes.bfloat16)).reshape(k // 32, 32, n)
    amax = np.abs(w).max(1)
    if fmt == "e4m3":
        byte = np.frexp(amax)[1] - 1 + 127 - 7
    else:
        mant, ex = np.frexp(amax / 6.0)
        byte = np.where(mant > 0.5, ex, ex - 1) + 127
    byte = np.clip(np.where(amax > 0, byte, 1), 1, 254)
    scaled = (w * np.exp2(127.0 - byte)[:, None, :]).reshape(k, n).astype(np.float32)
    by_word = np.ascontiguousarray(scaled.reshape(k // 512, 128, 4, n).transpose(0, 1, 3, 2))
    if fmt == "e4m3":
        words = by_word.astype(ml_dtypes.float8_e4m3fn).view(np.uint8)
    else:
        c = by_word.astype(ml_dtypes.float4_e2m1fn).view(np.uint8) & 0xF
        words = (c[..., 0::2] | (c[..., 1::2] << 4)).reshape(k // 512, 128, 2 * n)
    return np.ascontiguousarray(words), np.ascontiguousarray(byte.astype(np.uint8).reshape(k // 512, 16, n))


def unpack_weight(words, scales, fmt):
    g, _, n = scales.shape
    words = np.ascontiguousarray(words).reshape(g, 128, n, -1)
    if fmt == "e4m3":
        vals = words.view(ml_dtypes.float8_e4m3fn).astype(np.float64)
    else:
        nib = np.empty((g, 128, n, 4), np.uint8)
        nib[..., 0::2] = words & 0xF
        nib[..., 1::2] = words >> 4
        vals = E2M1[nib]
    vals = vals * np.repeat(np.exp2(scales.astype(np.float64) - 127.0), 8, axis=1)[..., None]
    return vals.transpose(0, 1, 3, 2).reshape(g * 512, n)


def sigmoid(v):
    return 1.0 / (1.0 + np.exp(-v))


K, T, J, N = 1024, 1024, 512, 512


def setup_inputs():
    n = np.random.standard_normal
    idx = np.random.permutation(T)[:J]
    idx2 = np.random.permutation(T)[:J]
    idx3 = np.random.permutation(T)[:J]
    fk = mx_kscale(K)
    xtp = pack_weight(n((K, T)) / fk[:, None], "e4m3")
    wbp = pack_weight(n((K, N)) * 1 / np.sqrt(K) * fk[:, None], "e2m1")
    wcp = pack_weight(n((K, N)) * 1 / np.sqrt(K) * fk[:, None], "e4m3")
    return {
        "xt_words": xtp[0],
        "xt_scales": xtp[1],
        "wa": (n((K, N)) * 1 / np.sqrt(K) * fk[:, None]).astype(np.float32),
        "wb_words": wbp[0],
        "wb_scales": wbp[1],
        "wc_words": wcp[0],
        "wc_scales": wcp[1],
        "offs": striped(idx),
        "offs2": striped(idx2),
        "offs3": striped(idx3),
    }


def reference(xt_words, xt_scales, wa, wb_words, wb_scales, wc_words, wc_scales, offs, offs2, offs3):
    idx = unstriped(offs)
    idx2 = unstriped(offs2)
    idx3 = unstriped(offs3)
    xtu = unpack_weight(xt_words, xt_scales, "e4m3")
    wbu = unpack_weight(wb_words, wb_scales, "e2m1")
    wcu = unpack_weight(wc_words, wc_scales, "e4m3")
    waq = mxq(f64(wa), 0, "e4m3")
    xtidxg = xtu[:, idx]
    xtidx2g = xtu[:, idx2]
    p = waq.T @ xtidxg + wbu.T @ xtidx2g
    xtidx3g = xtu[:, idx3]
    g = wcu.T @ xtidx3g
    y = p * sigmoid(g)
    return y

@@ -1,0 +1,172 @@
+from contextlib import ExitStack
+
+import concourse.mybir as mybir
+
+K, T, J, N = 1024, 1024, 512, 512
+FLOPS = 3 * 2 * K * N * J
+
+F32 = mybir.dt.float32
+BF16 = mybir.dt.bfloat16
+I32 = mybir.dt.int32
+U32 = mybir.dt.uint32
+U16 = mybir.dt.uint16
+U8 = mybir.dt.uint8
+FP8X4 = mybir.dt.float8_e4m3fn_x4
+FP4X4 = mybir.dt.float4_e2m1fn_x4
+
+P = 128
+PACK = 4
+PASSES = K // (P * PACK)
+QUADRANT = 32
+ROWS = 4
+TILES = N // P
+HALF = N // 2
+
+
+def tile_moe_two_experts_and_a_gate_kernel(
+    tc, xt_words, xt_scales, wa, wb_words, wb_scales, wc_words, wc_scales, offs, offs2, offs3, out
+):
+    nc = tc.nc
+    with ExitStack() as ctx:
+        keep = ctx.enter_context(tc.tile_pool(name="keep", bufs=1))
+        psum = ctx.enter_context(tc.psum_pool(name="psum", bufs=1))
+
+        list_a = keep.tile([P, J // 16], U16)
+        list_b = keep.tile([P, J // 16], U16)
+        list_c = keep.tile([P, J // 16], U16)
+        x_scales = keep.tile([P, T], U8, align_bytes=64)
+        x_words = keep.tile([P, PASSES, T], I32, align_bytes=64)
+        c_words = keep.tile([P, PASSES, N], I32, align_bytes=64)
+        c_scales = keep.tile([P, N], U8, align_bytes=64)
+        b_words = keep.tile([P, PASSES, 2 * N], U8, align_bytes=64)
+        b_scales = keep.tile([P, PASSES, N], U8, align_bytes=64)
+        a_words = keep.tile([P, PASSES, N], U32, align_bytes=64)
+        a_scales = keep.tile([P, PASSES, N], U8, align_bytes=64)
+        xb_scales_1 = keep.tile([P, J], U8, align_bytes=64)
+        raw_0a = keep.tile([P, PACK, HALF], F32)
+        raw_0b = keep.tile([P, PACK, HALF], F32)
+        raw_1a = keep.tile([P, PACK, HALF], F32)
+        raw_1b = keep.tile([P, PACK, HALF], F32, tag="reused")
+
+        nc.vector.memset(x_scales[:].bitcast(I32), 0)
+        nc.vector.memset(c_scales[:].bitcast(I32), 0)
+        nc.vector.memset(b_scales[:].bitcast(I32), 0)
+        nc.vector.memset(xb_scales_1[:].bitcast(I32), 0)
+
+        nc.sync.dma_start(list_b[:], offs2)
+        for q in range(P // QUADRANT):
+            (nc.sync, nc.scalar)[q % 2].dma_start(
+                x_scales[QUADRANT * q : QUADRANT * q + PASSES * ROWS, :].bitcast(I32),
+                xt_scales.bitcast(I32)[:, ROWS * q : ROWS * (q + 1), :],
+            )
+        nc.sync.dma_start(list_c[:], offs3)
+        nc.sync.dma_start(list_a[:], offs)
+        warm_in = keep.tile([P, 1], F32)
+        warm_out = keep.tile([P, 1], F32)
+        nc.gpsimd.memset(warm_in[:], 0.0)
+        nc.scalar.activation(warm_out[:], warm_in[:], mybir.ActivationFunctionType.Sigmoid)
+        nc.sync.dma_start(x_words[:], xt_words.rearrange("z p t r -> p z (t r)").bitcast(I32))
+        wa_rows = wa.rearrange("(z p r) n -> z p r n", z=PASSES, r=PACK)
+        nc.sync.dma_start(c_words[:], wc_words.rearrange("z p n r -> p z (n r)").bitcast(I32))
+        for q in range(P // QUADRANT):
+            nc.sync.dma_start(
+                c_scales[QUADRANT * q : QUADRANT * q + PASSES * ROWS, :].bitcast(I32),
+                wc_scales.bitcast(I32)[:, ROWS * q : ROWS * (q + 1), :],
+            )
+        nc.sync.dma_start(raw_0a[:], wa_rows[0][:, :, :HALF])
+        nc.sync.dma_start(b_words[:].bitcast(I32), wb_words.rearrange("z p c -> p z c").bitcast(I32))
+        nc.sync.dma_start(raw_1a[:], wa_rows[1][:, :, :HALF])
+        for q in range(P // QUADRANT):
+            nc.sync.dma_start(
+                b_scales[QUADRANT * q : QUADRANT * q + ROWS, :, :].bitcast(I32),
+                wb_scales.bitcast(I32)[:, ROWS * q : ROWS * (q + 1), :].rearrange("z r c -> r z c"),
+            )
+        nc.sync.dma_start(raw_0b[:], wa_rows[0][:, :, HALF:])
+        nc.sync.dma_start(raw_1b[:], wa_rows[1][:, :, HALF:])
+
+        def gather_scales(name, offsets):
+            picked = keep.tile([P, J], U8, name=name, align_bytes=64)
+            nc.vector.tensor_copy(picked[:], x_scales[:].indirect(offsets[:]))
+            return picked
+
+        def gather_words(name, z, offsets):
+            picked = keep.tile([P, J], U32, name=name, align_bytes=64)
+            nc.vector.tensor_copy(picked[:], x_words[:, z, :].bitcast(U32).indirect(offsets[:]))
+            return picked
+
+        xb_scales = gather_scales("xb_scales", list_b)
+        span = P - QUADRANT + ROWS
+        nc.sync.dma_start(xb_scales_1[:span, :].bitcast(I32), xb_scales[ROWS : ROWS + span, :].bitcast(I32))
+        xc_scales = gather_scales("xc_scales", list_c)
+        xa_scales = gather_scales("xa_scales", list_a)
+        xc_words = [gather_words("xc_words%d" % z, z, list_c) for z in range(PASSES)]
+        xb_words, xa_words = [], []
+        for z in range(PASSES):
+            xb_words.append(gather_words("xb_words%d" % z, z, list_b))
+            xa_words.append(gather_words("xa_words%d" % z, z, list_a))
+
+        def quantise(name, raw, z, n0, width):
+            grouped = keep.tile([P, width, PACK], BF16, name=name, align_bytes=64)
+            nc.scalar.copy(
+                grouped[:].rearrange("p (c i) r -> p c r i", i=4),
+                raw[:].rearrange("p r (c i) -> p c r i", i=4),
+            )
+            nc.vector.quantize_mx(
+                out=a_words[:, z, n0 : n0 + width].bitcast(FP8X4),
+                scales=a_scales[:, z, n0 : n0 + width],
+                in_=grouped[:].rearrange("p c r -> p (c r)"),
+            )
+
+        quantise("grouped_0a", raw_0a, 0, 0, HALF)
+        quantise("grouped_1a", raw_1a, 1, 0, HALF)
+        quantise("grouped_0b", raw_0b, 0, HALF, HALF)
+        quantise("grouped_1b", raw_1b, 1, HALF, HALF)
+
+        g_banks = [psum.tile([P, J], F32, name="g%d" % i) for i in range(TILES)]
+        p_banks = [psum.tile([P, J], F32, name="p%d" % i) for i in range(TILES)]
+        cols = [slice(P * i, P * (i + 1)) for i in range(TILES)]
+
+        for z in range(PASSES):
+            for i in range(TILES):
+                nc.tensor.matmul_mx(
+                    out=g_banks[i][:],
+                    lhsT=c_words[:, z, cols[i]].bitcast(FP8X4),
+                    lhsT_scale=c_scales[ROWS * z :, cols[i]],
+                    rhs=xc_words[z][:].bitcast(FP8X4),
+                    rhs_scale=xc_scales[ROWS * z :, :],
+                    start=(z == 0),
+                    stop=(z == PASSES - 1),
+                )
+        for z in range(PASSES):
+            for i in range(TILES):
+                nc.tensor.matmul_mx(
+                    out=p_banks[i][:],
+                    lhsT=b_words[:, z, 2 * P * i : 2 * P * (i + 1)].bitcast(FP4X4),
+                    lhsT_scale=b_scales[:, z, cols[i]],
+                    rhs=xb_words[z][:].bitcast(FP8X4),
+                    rhs_scale=(xb_scales, xb_scales_1)[z][:],
+                    start=(z == 0),
+                    stop=False,
+                )
+        for i in range(TILES):
+            for z in range(PASSES):
+                nc.tensor.matmul_mx(
+                    out=p_banks[i][:],
+                    lhsT=a_words[:, z, cols[i]].bitcast(FP8X4),
+                    lhsT_scale=a_scales[:, z, cols[i]],
+                    rhs=xa_words[z][:].bitcast(FP8X4),
+                    rhs_scale=xa_scales[ROWS * z :, :],
+                    start=False,
+                    stop=(z == PASSES - 1),
+                )
+
+        gate = keep.tile([P, TILES, J], F32, tag="reused")
+        for i in range(TILES):
+            nc.scalar.activation(gate[:, i, :], g_banks[i][:], mybir.ActivationFunctionType.Sigmoid)
+        for i in range(TILES):
+            result = keep.tile([P, J], F32, name="result%d" % i)
+            for j0, j1 in ((0, J - P), (J - P, J)) if i == TILES - 1 else ((0, J),):
+                nc.vector.tensor_tensor(
+                    result[:, j0:j1], p_banks[i][:, j0:j1], gate[:, i, j0:j1], mybir.AluOpType.mult
+                )
+                nc.sync.dma_start(out[cols[i], j0:j1], result[:, j0:j1])

@@ -46,12 +46,22 @@ def tile_moe_two_experts_and_a_gate_kernel(
         raw_0a = keep.tile([P, PACK, HALF], F32)
         raw_0b = keep.tile([P, PACK, HALF], F32)
         raw_1a = keep.tile([P, PACK, HALF], F32)
-        raw_1b = keep.tile([P, PACK, HALF], F32, tag="reused")
+        raw_1b = keep.tile([P, PACK, HALF], F32, tag="late_gates")
 
         nc.vector.memset(x_scales[:].bitcast(I32), 0)
         nc.vector.memset(c_scales[:].bitcast(I32), 0)
         nc.vector.memset(b_scales[:].bitcast(I32), 0)
         nc.vector.memset(xb_scales_1[:].bitcast(I32), 0)
+
+        def gather_scales(name, offsets):
+            picked = keep.tile([P, J], U8, name=name, align_bytes=64)
+            nc.vector.tensor_copy(picked[:], x_scales[:].indirect(offsets[:]))
+            return picked
+
+        def gather_words(name, z, offsets):
+            picked = keep.tile([P, J], U32, name=name, tag=name, align_bytes=64)
+            nc.vector.tensor_copy(picked[:], x_words[:, z, :].bitcast(U32).indirect(offsets[:]))
+            return picked
 
         nc.sync.dma_start(list_b[:], offs2)
         for q in range(P // QUADRANT):
@@ -60,22 +70,18 @@ def tile_moe_two_experts_and_a_gate_kernel(
                 xt_scales.bitcast(I32)[:, ROWS * q : ROWS * (q + 1), :],
             )
         nc.sync.dma_start(list_c[:], offs3)
-        nc.sync.dma_start(list_a[:], offs)
-        warm_in = keep.tile([P, 1], F32)
-        warm_out = keep.tile([P, 1], F32)
-        nc.gpsimd.memset(warm_in[:], 0.0)
-        nc.scalar.activation(warm_out[:], warm_in[:], mybir.ActivationFunctionType.Sigmoid)
         nc.sync.dma_start(x_words[:], xt_words.rearrange("z p t r -> p z (t r)").bitcast(I32))
         wa_rows = wa.rearrange("(z p r) n -> z p r n", z=PASSES, r=PACK)
+        nc.sync.dma_start(raw_0a[:], wa_rows[0][:, :, :HALF])
         nc.sync.dma_start(c_words[:], wc_words.rearrange("z p n r -> p z (n r)").bitcast(I32))
+        nc.sync.dma_start(list_a[:], offs)
         for q in range(P // QUADRANT):
             nc.sync.dma_start(
                 c_scales[QUADRANT * q : QUADRANT * q + PASSES * ROWS, :].bitcast(I32),
                 wc_scales.bitcast(I32)[:, ROWS * q : ROWS * (q + 1), :],
             )
-        nc.sync.dma_start(raw_0a[:], wa_rows[0][:, :, :HALF])
-        nc.sync.dma_start(b_words[:].bitcast(I32), wb_words.rearrange("z p c -> p z c").bitcast(I32))
         nc.sync.dma_start(raw_1a[:], wa_rows[1][:, :, :HALF])
+        nc.sync.dma_start(b_words[:].bitcast(I32), wb_words.bitcast(I32).rearrange("z p c -> p z c"))
         for q in range(P // QUADRANT):
             nc.sync.dma_start(
                 b_scales[QUADRANT * q : QUADRANT * q + ROWS, :, :].bitcast(I32),
@@ -83,30 +89,15 @@ def tile_moe_two_experts_and_a_gate_kernel(
             )
         nc.sync.dma_start(raw_0b[:], wa_rows[0][:, :, HALF:])
         nc.sync.dma_start(raw_1b[:], wa_rows[1][:, :, HALF:])
-
-        def gather_scales(name, offsets):
-            picked = keep.tile([P, J], U8, name=name, align_bytes=64)
-            nc.vector.tensor_copy(picked[:], x_scales[:].indirect(offsets[:]))
-            return picked
-
-        def gather_words(name, z, offsets):
-            picked = keep.tile([P, J], U32, name=name, align_bytes=64)
-            nc.vector.tensor_copy(picked[:], x_words[:, z, :].bitcast(U32).indirect(offsets[:]))
-            return picked
-
         xb_scales = gather_scales("xb_scales", list_b)
         span = P - QUADRANT + ROWS
         nc.sync.dma_start(xb_scales_1[:span, :].bitcast(I32), xb_scales[ROWS : ROWS + span, :].bitcast(I32))
-        xc_scales = gather_scales("xc_scales", list_c)
-        xa_scales = gather_scales("xa_scales", list_a)
-        xc_words = [gather_words("xc_words%d" % z, z, list_c) for z in range(PASSES)]
-        xb_words, xa_words = [], []
-        for z in range(PASSES):
-            xb_words.append(gather_words("xb_words%d" % z, z, list_b))
-            xa_words.append(gather_words("xa_words%d" % z, z, list_a))
 
-        def quantise(name, raw, z, n0, width):
-            grouped = keep.tile([P, width, PACK], BF16, name=name, align_bytes=64)
+        xc_scales = gather_scales("xc_scales", list_c)
+        xc_words = [gather_words("xc_words%d" % z, z, list_c) for z in range(PASSES)]
+        xa_scales = gather_scales("xa_scales", list_a)
+        def quantise(name, raw, z, n0, width, tag):
+            grouped = keep.tile([P, width, PACK], BF16, name=name, tag=tag, align_bytes=64)
             nc.scalar.copy(
                 grouped[:].rearrange("p (c i) r -> p c r i", i=4),
                 raw[:].rearrange("p r (c i) -> p c r i", i=4),
@@ -117,17 +108,21 @@ def tile_moe_two_experts_and_a_gate_kernel(
                 in_=grouped[:].rearrange("p c r -> p (c r)"),
             )
 
-        quantise("grouped_0a", raw_0a, 0, 0, HALF)
-        quantise("grouped_1a", raw_1a, 1, 0, HALF)
-        quantise("grouped_0b", raw_0b, 0, HALF, HALF)
-        quantise("grouped_1b", raw_1b, 1, HALF, HALF)
+        xb_words = [gather_words("xb_words0", 0, list_b)]
+        xa_words = [gather_words("xa_words0", 0, list_a)]
+        xb_words.append(gather_words("xb_words1", 1, list_b))
+        xa_words.append(gather_words("xa_words1", 1, list_a))
+        quantise("grouped_0a", raw_0a, 0, 0, HALF, "grouped_0a")
+        quantise("grouped_1a", raw_1a, 1, 0, HALF, "grouped_1a")
+        quantise("grouped_0b", raw_0b, 0, HALF, HALF, "grouped_0b")
+        quantise("grouped_1b", raw_1b, 1, HALF, HALF, "grouped_1b")
 
         g_banks = [psum.tile([P, J], F32, name="g%d" % i) for i in range(TILES)]
         p_banks = [psum.tile([P, J], F32, name="p%d" % i) for i in range(TILES)]
         cols = [slice(P * i, P * (i + 1)) for i in range(TILES)]
 
-        for z in range(PASSES):
-            for i in range(TILES):
+        for i in range(TILES):
+            for z in range(PASSES):
                 nc.tensor.matmul_mx(
                     out=g_banks[i][:],
                     lhsT=c_words[:, z, cols[i]].bitcast(FP8X4),
@@ -160,13 +155,15 @@ def tile_moe_two_experts_and_a_gate_kernel(
                     stop=(z == PASSES - 1),
                 )
 
-        gate = keep.tile([P, TILES, J], F32, tag="reused")
+        first_gate = keep.tile([P, J], F32)
+        late_gates = keep.tile([P, TILES - 1, J], F32, tag="late_gates")
+        gate = [first_gate[:]] + [late_gates[:, i, :] for i in range(TILES - 1)]
         for i in range(TILES):
-            nc.scalar.activation(gate[:, i, :], g_banks[i][:], mybir.ActivationFunctionType.Sigmoid)
+            nc.scalar.activation(gate[i], g_banks[i][:], mybir.ActivationFunctionType.Sigmoid)
         for i in range(TILES):
             result = keep.tile([P, J], F32, name="result%d" % i)
-            for j0, j1 in ((0, J - P), (J - P, J)) if i == TILES - 1 else ((0, J),):
+            for j0, j1 in ((0, J // 2), (J // 2, J)) if i in (0, TILES - 1) else ((0, J),):
                 nc.vector.tensor_tensor(
-                    result[:, j0:j1], p_banks[i][:, j0:j1], gate[:, i, j0:j1], mybir.AluOpType.mult
+                    result[:, j0:j1], p_banks[i][:, j0:j1], gate[i][:, j0:j1], mybir.AluOpType.mult
                 )
                 nc.sync.dma_start(out[cols[i], j0:j1], result[:, j0:j1])

from contextlib import ExitStack

import concourse.mybir as mybir

K, T, J, N = 1024, 1024, 512, 512
FLOPS = 3 * 2 * K * N * J

F32 = mybir.dt.float32
BF16 = mybir.dt.bfloat16
I32 = mybir.dt.int32
U32 = mybir.dt.uint32
U16 = mybir.dt.uint16
U8 = mybir.dt.uint8
FP8X4 = mybir.dt.float8_e4m3fn_x4
FP4X4 = mybir.dt.float4_e2m1fn_x4

P = 128
PACK = 4
PASSES = K // (P * PACK)
QUADRANT = 32
ROWS = 4
TILES = N // P
HALF = N // 2


def tile_moe_two_experts_and_a_gate_kernel(
    tc, xt_words, xt_scales, wa, wb_words, wb_scales, wc_words, wc_scales, offs, offs2, offs3, out
):
    nc = tc.nc
    with ExitStack() as ctx:
        keep = ctx.enter_context(tc.tile_pool(name="keep", bufs=1))
        psum = ctx.enter_context(tc.psum_pool(name="psum", bufs=1))

        list_a = keep.tile([P, J // 16], U16)
        list_b = keep.tile([P, J // 16], U16)
        list_c = keep.tile([P, J // 16], U16)
        x_scales = keep.tile([P, T], U8, align_bytes=64)
        x_words = keep.tile([P, PASSES, T], I32, align_bytes=64)
        c_words = keep.tile([P, PASSES, N], I32, align_bytes=64)
        c_scales = keep.tile([P, N], U8, align_bytes=64)
        b_words = keep.tile([P, PASSES, 2 * N], U8, align_bytes=64)
        b_scales = keep.tile([P, PASSES, N], U8, align_bytes=64)
        a_words = keep.tile([P, PASSES, N], U32, align_bytes=64)
        a_scales = keep.tile([P, PASSES, N], U8, align_bytes=64)
        xb_scales_1 = keep.tile([P, J], U8, align_bytes=64)
        raw_0a = keep.tile([P, PACK, HALF], F32)
        raw_0b = keep.tile([P, PACK, HALF], F32)
        raw_1a = keep.tile([P, PACK, HALF], F32)
        raw_1b = keep.tile([P, PACK, HALF], F32, tag="late_gates")

        nc.vector.memset(x_scales[:].bitcast(I32), 0)
        nc.vector.memset(c_scales[:].bitcast(I32), 0)
        nc.vector.memset(b_scales[:].bitcast(I32), 0)
        nc.vector.memset(xb_scales_1[:].bitcast(I32), 0)

        def gather_scales(name, offsets):
            picked = keep.tile([P, J], U8, name=name, align_bytes=64)
            nc.vector.tensor_copy(picked[:], x_scales[:].indirect(offsets[:]))
            return picked

        def gather_words(name, z, offsets):
            picked = keep.tile([P, J], U32, name=name, tag=name, align_bytes=64)
            nc.vector.tensor_copy(picked[:], x_words[:, z, :].bitcast(U32).indirect(offsets[:]))
            return picked

        nc.sync.dma_start(list_b[:], offs2)
        for q in range(P // QUADRANT):
            (nc.sync, nc.scalar)[q % 2].dma_start(
                x_scales[QUADRANT * q : QUADRANT * q + PASSES * ROWS, :].bitcast(I32),
                xt_scales.bitcast(I32)[:, ROWS * q : ROWS * (q + 1), :],
            )
        nc.sync.dma_start(list_c[:], offs3)
        nc.sync.dma_start(x_words[:], xt_words.rearrange("z p t r -> p z (t r)").bitcast(I32))
        wa_rows = wa.rearrange("(z p r) n -> z p r n", z=PASSES, r=PACK)
        nc.sync.dma_start(raw_0a[:], wa_rows[0][:, :, :HALF])
        nc.sync.dma_start(c_words[:], wc_words.rearrange("z p n r -> p z (n r)").bitcast(I32))
        nc.sync.dma_start(list_a[:], offs)
        for q in range(P // QUADRANT):
            nc.sync.dma_start(
                c_scales[QUADRANT * q : QUADRANT * q + PASSES * ROWS, :].bitcast(I32),
                wc_scales.bitcast(I32)[:, ROWS * q : ROWS * (q + 1), :],
            )
        nc.sync.dma_start(raw_1a[:], wa_rows[1][:, :, :HALF])
        nc.sync.dma_start(b_words[:].bitcast(I32), wb_words.bitcast(I32).rearrange("z p c -> p z c"))
        for q in range(P // QUADRANT):
            nc.sync.dma_start(
                b_scales[QUADRANT * q : QUADRANT * q + ROWS, :, :].bitcast(I32),
                wb_scales.bitcast(I32)[:, ROWS * q : ROWS * (q + 1), :].rearrange("z r c -> r z c"),
            )
        nc.sync.dma_start(raw_0b[:], wa_rows[0][:, :, HALF:])
        nc.sync.dma_start(raw_1b[:], wa_rows[1][:, :, HALF:])
        xb_scales = gather_scales("xb_scales", list_b)
        span = P - QUADRANT + ROWS
        nc.sync.dma_start(xb_scales_1[:span, :].bitcast(I32), xb_scales[ROWS : ROWS + span, :].bitcast(I32))

        xc_scales = gather_scales("xc_scales", list_c)
        xc_words = [gather_words("xc_words%d" % z, z, list_c) for z in range(PASSES)]
        xa_scales = gather_scales("xa_scales", list_a)
        def quantise(name, raw, z, n0, width, tag):
            grouped = keep.tile([P, width, PACK], BF16, name=name, tag=tag, align_bytes=64)
            nc.scalar.copy(
                grouped[:].rearrange("p (c i) r -> p c r i", i=4),
                raw[:].rearrange("p r (c i) -> p c r i", i=4),
            )
            nc.vector.quantize_mx(
                out=a_words[:, z, n0 : n0 + width].bitcast(FP8X4),
                scales=a_scales[:, z, n0 : n0 + width],
                in_=grouped[:].rearrange("p c r -> p (c r)"),
            )

        xb_words = [gather_words("xb_words0", 0, list_b)]
        xa_words = [gather_words("xa_words0", 0, list_a)]
        xb_words.append(gather_words("xb_words1", 1, list_b))
        xa_words.append(gather_words("xa_words1", 1, list_a))
        quantise("grouped_0a", raw_0a, 0, 0, HALF, "grouped_0a")
        quantise("grouped_1a", raw_1a, 1, 0, HALF, "grouped_1a")
        quantise("grouped_0b", raw_0b, 0, HALF, HALF, "grouped_0b")
        quantise("grouped_1b", raw_1b, 1, HALF, HALF, "grouped_1b")

        g_banks = [psum.tile([P, J], F32, name="g%d" % i) for i in range(TILES)]
        p_banks = [psum.tile([P, J], F32, name="p%d" % i) for i in range(TILES)]
        cols = [slice(P * i, P * (i + 1)) for i in range(TILES)]

        for i in range(TILES):
            for z in range(PASSES):
                nc.tensor.matmul_mx(
                    out=g_banks[i][:],
                    lhsT=c_words[:, z, cols[i]].bitcast(FP8X4),
                    lhsT_scale=c_scales[ROWS * z :, cols[i]],
                    rhs=xc_words[z][:].bitcast(FP8X4),
                    rhs_scale=xc_scales[ROWS * z :, :],
                    start=(z == 0),
                    stop=(z == PASSES - 1),
                )
        for z in range(PASSES):
            for i in range(TILES):
                nc.tensor.matmul_mx(
                    out=p_banks[i][:],
                    lhsT=b_words[:, z, 2 * P * i : 2 * P * (i + 1)].bitcast(FP4X4),
                    lhsT_scale=b_scales[:, z, cols[i]],
                    rhs=xb_words[z][:].bitcast(FP8X4),
                    rhs_scale=(xb_scales, xb_scales_1)[z][:],
                    start=(z == 0),
                    stop=False,
                )
        for i in range(TILES):
            for z in range(PASSES):
                nc.tensor.matmul_mx(
                    out=p_banks[i][:],
                    lhsT=a_words[:, z, cols[i]].bitcast(FP8X4),
                    lhsT_scale=a_scales[:, z, cols[i]],
                    rhs=xa_words[z][:].bitcast(FP8X4),
                    rhs_scale=xa_scales[ROWS * z :, :],
                    start=False,
                    stop=(z == PASSES - 1),
                )

        first_gate = keep.tile([P, J], F32)
        late_gates = keep.tile([P, TILES - 1, J], F32, tag="late_gates")
        gate = [first_gate[:]] + [late_gates[:, i, :] for i in range(TILES - 1)]
        for i in range(TILES):
            nc.scalar.activation(gate[i], g_banks[i][:], mybir.ActivationFunctionType.Sigmoid)
        for i in range(TILES):
            result = keep.tile([P, J], F32, name="result%d" % i)
            for j0, j1 in ((0, J // 2), (J // 2, J)) if i in (0, TILES - 1) else ((0, J),):
                nc.vector.tensor_tensor(
                    result[:, j0:j1], p_banks[i][:, j0:j1], gate[i][:, j0:j1], mybir.AluOpType.mult
                )
                nc.sync.dma_start(out[cols[i], j0:j1], result[:, j0:j1])
